import numpy as np
import ml_dtypes


def mxq(x, axis, fmt="e4m3"):
    dtype, down = {"e4m3": (ml_dtypes.float8_e4m3fn, 7), "e5m2": (ml_dtypes.float8_e5m2, 14)}[fmt]
    v = np.moveaxis(np.asarray(x, np.float32).astype(ml_dtypes.bfloat16).astype(np.float64), axis, -1)
    blocks = v.reshape(v.shape[:-1] + (-1, 32))
    amax = np.abs(blocks).max(-1, keepdims=True)
    byte = np.maximum(np.where(amax > 0, np.frexp(amax)[1] - 1 + 127, 0) - down, 1)
    scale = np.exp2(byte - 127.0)
    codes = (blocks / scale).astype(np.float32).astype(dtype).astype(np.float64)
    return np.moveaxis((codes * scale).reshape(v.shape), -1, axis)


WIDE = False


def mx_kscale(k):
    if not WIDE:
        return np.ones(k)
    levels = np.array([10, -10, 5, -5, 0])
    if k % 512:
        return np.exp2(np.random.permutation(np.resize(levels, k // 32))).repeat(32)
    a = np.empty((k // 512, 16))
    for p in range(k // 512):
        a[p, :8] = np.random.permutation(np.resize(levels, 8))
        for g in range(8):
            far = levels[np.abs(levels - a[p, g]) >= 10]
            a[p, g + 8] = far[np.random.randint(len(far))]
    return np.exp2(a.ravel()).repeat(32)


def f64(x):
    return np.asarray(x).astype(np.float64)


def striped(idx):
    return np.tile(idx.reshape(-1, 16).T, (8, 1)).astype(np.uint16)


def unstriped(offs):
    return offs[:16].T.reshape(-1).astype(np.int64)


def pack_weight(w):
    k, n = w.shape
    w = f64(np.asarray(w, np.float32).astype(ml_dtypes.bfloat16)).reshape(k // 32, 32, n)
    amax = np.abs(w).max(1)
    byte = np.clip(np.where(amax > 0, np.frexp(amax)[1] - 1 + 127 - 7, 1), 1, 254)
    scaled = (w * np.exp2(127.0 - byte)[:, None, :]).reshape(k, n).astype(np.float32)
    words = np.ascontiguousarray(scaled.reshape(k // 512, 128, 4, n).transpose(0, 1, 3, 2)).astype(ml_dtypes.float8_e4m3fn).view(np.uint8)
    return words, np.ascontiguousarray(byte.astype(np.uint8).reshape(k // 512, 16, n))


def unpack_weight(words, scales):
    g, p, n, _ = words.shape
    vals = np.ascontiguousarray(words).view(ml_dtypes.float8_e4m3fn).astype(np.float64) * np.repeat(np.exp2(scales.astype(np.float64) - 127.0), 8, axis=1)[..., None]
    return vals.transpose(0, 1, 3, 2).reshape(g * 512, n)


E2M1 = np.array([0.0, 0.5, 1.0, 1.5, 2.0, 3.0, 4.0, 6.0, -0.0, -0.5, -1.0, -1.5, -2.0, -3.0, -4.0, -6.0])


def pack_fp4(w):
    k, n = w.shape
    w = f64(np.asarray(w, np.float32).astype(ml_dtypes.bfloat16)).reshape(k // 32, 32, n)
    amax = np.abs(w).max(1)
    mant, ex = np.frexp(amax / 6.0)
    byte = np.clip(np.where(amax > 0, np.where(mant > 0.5, ex, ex - 1) + 127, 1), 1, 254)
    scaled = (w * np.exp2(127.0 - byte)[:, None, :]).reshape(k, n).astype(np.float32)
    c = np.ascontiguousarray(scaled.reshape(k // 512, 128, 4, n).transpose(0, 1, 3, 2)).astype(ml_dtypes.float4_e2m1fn).view(np.uint8) & 0xF
    words = (c[..., 0::2] | (c[..., 1::2] << 4)).reshape(k // 512, 128, 2 * n)
    return np.ascontiguousarray(words), np.ascontiguousarray(byte.astype(np.uint8).reshape(k // 512, 16, n))


def unpack_fp4(words, scales):
    g, _, n = scales.shape
    words = np.ascontiguousarray(words).reshape(g, 128, n, 2)
    nib = np.empty((g, 128, n, 4), np.uint8)
    nib[..., 0::2] = words & 0xF
    nib[..., 1::2] = words >> 4
    vals = E2M1[nib] * np.repeat(np.exp2(scales.astype(np.float64) - 127.0), 8, axis=1)[..., None]
    return vals.transpose(0, 1, 3, 2).reshape(g * 512, n)


K, T, S, N, H, U = 512, 2048, 512, 256, 512, 1024


def setup_inputs():
    n = np.random.standard_normal
    s = mx_kscale(K)[:, None]
    u = mx_kscale(H)
    packed_xT = pack_weight(n((K, T)) * s)
    packed_w1 = pack_fp4(n((K, H)) / np.sqrt(K) / s)
    packed_w2 = pack_fp4(n((K, H)) / np.sqrt(K) / s)
    packed_w3 = pack_fp4(n((H, N)) / np.sqrt(H) / u[:, None])
    return {
        "x_words": packed_xT[0],
        "x_scales": packed_xT[1],
        "w1_words": packed_w1[0],
        "w1_scales": packed_w1[1],
        "w2_words": packed_w2[0],
        "w2_scales": packed_w2[1],
        "dist": (np.random.uniform(0.6, 2.5, (H, U))).astype(np.float32),
        "unit": (np.random.uniform(0.6, 1.4, (H, 1)) * u[:, None]).astype(np.float32),
        "w3_words": packed_w3[0],
        "w3_scales": packed_w3[1],
        "offs": striped(np.random.permutation(T)[:S]),
        "pi": striped(np.random.permutation(np.concatenate([np.arange(S), np.random.randint(0, S, U - S)]))),
        "pj": striped(np.random.permutation(np.concatenate([np.arange(S), np.random.randint(0, S, U - S)]))),
    }


def reference(x_words, x_scales, w1_words, w1_scales, w2_words, w2_scales, dist, unit, w3_words, w3_scales, offs, pi, pj):
    xq = unpack_weight(x_words, x_scales)[:, unstriped(offs)]
    chg = unpack_fp4(w1_words, w1_scales).T @ xq
    qi = chg[:, unstriped(pi)]
    qj = chg[:, unstriped(pj)]
    damp = (np.exp(-1.0 * ((0.8 * f64(dist)) ** 2))) / f64(dist)
    cou = (qi * qj) * damp
    pol = unpack_fp4(w2_words, w2_scales).T @ xq
    alpha = np.log(np.exp(pol) + 1.0)
    al_i = alpha[:, unstriped(pi)]
    alij = np.sqrt(al_i * alpha[:, unstriped(pj)] + 0.1)
    sw = (-1.0 * f64(dist) + 2.5) / (alij + 0.6)
    hid = f64(unit) * (cou * sw)
    return unpack_fp4(w3_words, w3_scales).T @ mxq(hid, 0, "e4m3")

import math
from contextlib import ExitStack

import concourse.mybir as mybir

K, T, S, N, H, U = 512, 2048, 512, 256, 512, 1024
FLOPS = 2 * (2 * K * H * S + H * N * U)

F32 = mybir.dt.float32
BF16 = mybir.dt.bfloat16
I32 = mybir.dt.int32
U32 = mybir.dt.uint32
U16 = mybir.dt.uint16
U8 = mybir.dt.uint8
FP8X4 = mybir.dt.float8_e4m3fn_x4
FP4X4 = mybir.dt.float4_e2m1fn_x4
ACT = mybir.ActivationFunctionType
ALU = mybir.AluOpType

P = 128
PACK = 4
SPARE = U + 32 - S
CHUNK = 256
TINY = 1e-19


def tile_picked_yewald_sw_p_kernel(
    tc, x_words, x_scales, w1_words, w1_scales, w2_words, w2_scales, dist, unit, w3_words, w3_scales, offs, pi, pj, out
):
    nc = tc.nc
    with ExitStack() as ctx:
        keep = ctx.enter_context(tc.tile_pool(name="keep", bufs=1))
        psum = ctx.enter_context(tc.psum_pool(name="psum", bufs=1))

        def tile(name, width, dtype):
            return keep.tile([P, width], dtype, name=name, align_bytes=64)

        def load_words(dst, src, queue):
            queue.dma_start(out=dst[:].bitcast(I32), in_=src.bitcast(I32))

        def load_scales(dst, src, queue):
            for q in range(4):
                four = src[0, 4 * q : 4 * q + 4, :].bitcast(I32)
                queue.dma_start(out=dst[32 * q : 32 * q + 32, :].bitcast(I32), in_=four.unsqueeze(0).to_broadcast([8, 4, four.shape[1]]))

        offs_t = keep.tile([P, S // 16], U16, name="offs_t")
        pi_t = keep.tile([P, U // 16], U16, name="pi_t")
        pj_t = keep.tile([P, U // 16], U16, name="pj_t")
        xw = tile("xw", T, I32)
        xs = tile("xs", T, U8)
        w1w, w2w, w3w = tile("w1w", 2 * H, U8), tile("w2w", 2 * H, U8), tile("w3w", 2 * N, U8)
        w1s, w2s, w3s = tile("w1s", H, U8), tile("w2s", H, U8), tile("w3s", N, U8)
        d = tile("d", PACK * U, F32)
        unit_t = tile("unit_t", PACK, F32)
        dist_v = dist.rearrange("(p t) r -> p t r", t=PACK)


        def rows(t):
            return slice(t * U, (t + 1) * U)

        def load_dist(t):
            nc.sync.dma_start(out=d[:, rows(t)], in_=dist_v[:, t, :])

        load_dist(0)
        load_dist(1)
        nc.sync.dma_start(out=offs_t[:], in_=offs)
        load_words(w1w, w1_words[0], nc.sync)
        load_scales(xs, x_scales, nc.scalar)
        load_scales(w1s, w1_scales, nc.gpsimd)
        nc.sync.dma_start(out=xw[:], in_=x_words[0].rearrange("p n t -> p (n t)").bitcast(I32))
        nc.sync.dma_start(out=pi_t[:], in_=pi)
        nc.sync.dma_start(out=pj_t[:], in_=pj)
        load_dist(2)
        load_dist(3)
        nc.sync.dma_start(out=unit_t[:], in_=unit.rearrange("(p t) o -> p (t o)", t=PACK))
        load_words(w2w, w2_words[0], nc.sync)
        load_scales(w2s, w2_scales, nc.sync)
        load_words(w3w, w3_words[0], nc.sync)
        load_scales(w3s, w3_scales, nc.sync)

        chg = [tile("chg%d" % t, S + SPARE, F32) for t in range(PACK)]
        alpha = [tile("alpha%d" % t, S + SPARE, F32) for t in range(PACK)]
        for table in chg + alpha:
            nc.vector.memset(table[:, S:], 0.0)

        def deal(name, words, scales):
            words_d, scales_d = tile(name + "w_d", 2 * H, U8), tile(name + "s_d", H, U8)
            nc.vector.tensor_copy(
                out=words_d[:].rearrange("p (t m b) -> p t m b", t=PACK, b=2),
                in_=words[:].rearrange("p (m t b) -> p t m b", t=PACK, b=2),
            )
            nc.vector.tensor_copy(
                out=scales_d[:].rearrange("p (t m) -> p t m", t=PACK),
                in_=scales[:].rearrange("p (m t) -> p t m", t=PACK),
            )
            return words_d, scales_d

        xgw, xgs = tile("xgw", S, U32), tile("xgs", S, U8)

        def first_product(words_d, scales_d, t, bank):
            acc = psum.tile([P, S], F32, name="bank%d" % bank)
            nc.tensor.matmul_mx(
                out=acc[:],
                lhsT=words_d[:, 2 * P * t : 2 * P * (t + 1)].bitcast(FP4X4),
                lhsT_scale=scales_d[:, P * t : P * (t + 1)],
                rhs=xgw[:].bitcast(FP8X4),
                rhs_scale=xgs[:],
                start=True,
                stop=True,
            )
            return acc

        w1w_d, w1s_d = deal("w1", w1w, w1s)
        nc.vector.tensor_copy(xgs[:], xs[:].indirect(offs_t[:]))
        nc.vector.tensor_copy(xgw[:], xw[:].bitcast(U32).indirect(offs_t[:]))
        chg_ps = [first_product(w1w_d, w1s_d, t, t) for t in range(PACK)]

        sq = tile("sq", PACK * U, F32)
        gauss = tile("gauss", PACK * U, F32)
        left = tile("left", (PACK - 1) * U, F32)
        al_i = tile("al_i", PACK * U, F32)
        prod = tile("prod", PACK * U, F32)
        soft = tile("soft", PACK * S, F32)
        neg_unit = tile("neg_unit", PACK, F32)
        nc.vector.tensor_scalar(neg_unit[:], unit_t[:], -1.0, None, ALU.mult)

        def columns(buf, first, width):
            return buf[:].rearrange("p (t r) -> p t r", t=PACK)[:, :, first : first + width]

        def charges(t):
            between = soft[:, 2 * S :] if t == PACK - 1 else left[:, rows(t)]
            nc.vector.tensor_tensor(between, chg[t][:].indirect(pi_t[:]), d[:, rows(t)], ALU.mult)
            nc.vector.tensor_tensor(d[:, rows(t)], chg[t][:].indirect(pj_t[:]), between, ALU.mult)

        def over_dist(t):
            nc.vector.scalar_tensor_tensor(gauss[:, rows(t)], d[:, rows(t)], neg_unit[:, t : t + 1], sq[:, rows(t)], ALU.mult, ALU.mult)

        for t in range(PACK):
            nc.scalar.activation(sq[:, rows(t)], d[:, rows(t)], ACT.Square)
            nc.scalar.activation(gauss[:, rows(t)], sq[:, rows(t)], ACT.Exp, bias=math.log(1.0 / 0.6), scale=-0.64)
            nc.vector.scalar_tensor_tensor(d[:, rows(t)], d[:, rows(t)], 2.5, gauss[:, rows(t)], ALU.subtract, ALU.mult)
            if t == 0:
                nc.vector.tensor_copy(chg[t][:, :S], chg_ps[t][:])
            else:
                nc.scalar.copy(chg[t][:, :S], chg_ps[t][:])
        w2w_d, w2s_d = deal("w2", w2w, w2s)
        pol_ps = [first_product(w2w_d, w2s_d, t, PACK + t) for t in range(PACK)]
        for c in range(U // CHUNK):
            nc.scalar.activation(columns(sq, c * CHUNK, CHUNK), columns(sq, c * CHUNK, CHUNK), ACT.Abs_reciprocal_sqrt)
        sig = [columns(gauss, t * CHUNK, CHUNK)[:, 2:, :] for t in range(PACK)]
        for t in range(PACK):
            nc.scalar.activation(sig[t], pol_ps[t][:].rearrange("p (a r) -> p a r", a=2), ACT.Sigmoid, scale=-1.0)
        for t in range(PACK):
            nc.scalar.activation(soft[:, t * S : (t + 1) * S].rearrange("p (a r) -> p a r", a=2), sig[t], ACT.Ln, bias=TINY)
            nc.vector.scalar_tensor_tensor(alpha[t][:, :S], soft[:, t * S : (t + 1) * S], -1.0, pol_ps[t][:], ALU.mult, ALU.max)

        for t in range(PACK):
            nc.scalar.activation(al_i[:, rows(t)], alpha[t][:].indirect(pi_t[:]), ACT.Copy)
            nc.vector.tensor_tensor(prod[:, rows(t)], alpha[t][:].indirect(pj_t[:]), al_i[:, rows(t)], ALU.mult)
        for t in range(PACK):
            nc.scalar.activation(prod[:, rows(t)], prod[:, rows(t)], ACT.Ln, bias=0.1)
        for t in range(PACK):
            charges(t)
            over_dist(t)

        out_v = out.rearrange("(a p) r -> p a r", p=P)
        for c in range(U // CHUNK):
            first = c * CHUNK
            switch = columns(prod, first, CHUNK)
            nc.scalar.activation(switch, switch, ACT.Sigmoid, bias=math.log(0.6), scale=-0.5)
            hid = tile("hid%d" % c, PACK * CHUNK, BF16)
            nc.vector.tensor_tensor(
                hid[:].rearrange("p (g i t) -> p g t i", i=4, t=PACK),
                columns(gauss, first, CHUNK).rearrange("p t (g i) -> p g t i", i=4),
                switch.rearrange("p t (g i) -> p g t i", i=4),
                ALU.mult,
            )
            codes, scales = tile("codes%d" % c, CHUNK, U32), tile("scales%d" % c, CHUNK, U8)
            nc.vector.quantize_mx(out=codes[:].bitcast(FP8X4), scales=scales[:], in_=hid[:])
            acc = psum.tile([P, N // P, CHUNK], F32, name="bank%d" % c)
            for a in range(N // P):
                nc.tensor.matmul_mx(
                    out=acc[:, a, :],
                    lhsT=w3w[:, 2 * P * a : 2 * P * (a + 1)].bitcast(FP4X4),
                    lhsT_scale=w3s[:, P * a : P * (a + 1)],
                    rhs=codes[:].bitcast(FP8X4),
                    rhs_scale=scales[:],
                    start=True,
                    stop=True,
                )
            result = keep.tile([P, N // P, CHUNK], F32, name="result%d" % c)
            nc.scalar.copy(result[:], acc[:])
            nc.sync.dma_start(out=out_v[:, :, first : first + CHUNK], in_=result[:])
